import numpy as np
import ml_dtypes


def mxq(x, axis, fmt="e4m3"):
    dtype, down = {"e4m3": (ml_dtypes.float8_e4m3fn, 7), "e5m2": (ml_dtypes.float8_e5m2, 14)}[fmt]
    v = np.moveaxis(np.asarray(x, np.float32).astype(ml_dtypes.bfloat16).astype(np.float64), axis, -1)
    blocks = v.reshape(v.shape[:-1] + (-1, 32))
    amax = np.abs(blocks).max(-1, keepdims=True)
    byte = np.maximum(np.where(amax > 0, np.frexp(amax)[1] - 1 + 127, 0) - down, 1)
    scale = np.exp2(byte - 127.0)
    codes = (blocks / scale).astype(np.float32).astype(dtype).astype(np.float64)
    return np.moveaxis((codes * scale).reshape(v.shape), -1, axis)


WIDE = False


def mx_kscale(k):
    if not WIDE:
        return np.ones(k)
    levels = np.array([30, -30])
    if k % 512:
        return np.exp2(np.random.permutation(np.resize(levels, k // 32))).repeat(32)
    a = np.empty((k // 512, 16))
    for p in range(k // 512):
        a[p, :8] = np.random.permutation(np.resize(levels, 8))
        for g in range(8):
            far = levels[np.abs(levels - a[p, g]) >= 10]
            a[p, g + 8] = far[np.random.randint(len(far))]
    return np.exp2(a.ravel()).repeat(32)


BF16 = ml_dtypes.bfloat16


def bf(x):
    return np.asarray(x, np.float32).astype(BF16)


def f64(x):
    return np.asarray(x).astype(np.float64)


E2M1 = np.array([0.0, 0.5, 1.0, 1.5, 2.0, 3.0, 4.0, 6.0, -0.0, -0.5, -1.0, -1.5, -2.0, -3.0, -4.0, -6.0])


def pack_weight(w, fmt):
    k, n = w.shape
    w = f64(bf(w)).reshape(k // 32, 32, n)
    amax = np.abs(w).max(1)
    if fmt == "e4m3":
        byte = np.frexp(amax)[1] - 1 + 127 - 7
    else:
        mant, ex = np.frexp(amax / 6.0)
        byte = np.where(mant > 0.5, ex, ex - 1) + 127
    byte = np.clip(np.where(amax > 0, byte, 1), 1, 254)
    scaled = (w * np.exp2(127.0 - byte)[:, None, :]).reshape(k, n).astype(np.float32)
    by_word = np.ascontiguousarray(scaled.reshape(k // 512, 128, 4, n).transpose(0, 1, 3, 2))
    if fmt == "e4m3":
        words = by_word.astype(ml_dtypes.float8_e4m3fn).view(np.uint8)
    else:
        c = by_word.astype(ml_dtypes.float4_e2m1fn).view(np.uint8) & 0xF
        words = c[..., 0::2] | (c[..., 1::2] << 4)
    return np.ascontiguousarray(words), np.ascontiguousarray(byte.astype(np.uint8).reshape(k // 512, 16, n))


def unpack_weight(words, scales, fmt):
    g, p, n, _ = words.shape
    if fmt == "e4m3":
        vals = np.ascontiguousarray(words).view(ml_dtypes.float8_e4m3fn).astype(np.float64)
    else:
        nib = np.empty((g, p, n, 4), np.uint8)
        nib[..., 0::2] = words & 0xF
        nib[..., 1::2] = words >> 4
        vals = E2M1[nib]
    vals = vals * np.repeat(np.exp2(scales.astype(np.float64) - 127.0), 8, axis=1)[..., None]
    return vals.transpose(0, 1, 3, 2).reshape(g * 512, n)
def pack4(w):
    words, scales = pack_weight(w, "e2m1")
    return words.reshape(words.shape[0], 128, -1), scales


def unpack4(words, scales):
    return unpack_weight(words.reshape(words.shape[0], 128, -1, 2), scales, "e2m1")


M, H, R = 512, 2048, 1024


def setup_inputs():
    s = mx_kscale(H)
    t = mx_kscale(H)
    x = np.random.standard_normal((M, H)) * np.exp(0.5 * np.random.standard_normal((M, H)))
    contact = np.abs(np.random.standard_normal((H, H))) / np.sqrt(H)
    c_words, c_scales = pack4(contact / s[:, None] * t)
    return {
        "x": bf(x * s),
        "c_words": c_words,
        "c_scales": c_scales,
        "susceptible": bf(np.random.uniform(0.2, 1.0, (M, H))),
        "recovery": bf(np.random.uniform(0.3, 0.8, H) * t / s),
        "w": bf(np.random.standard_normal((H, R)) / np.sqrt(H) / t[:, None]),
        "b": bf(0.3 * np.random.standard_normal(R)),
    }


def reference(x, c_words, c_scales, susceptible, recovery, w, b):
    x = f64(x)
    force = mxq(x, 1, "e4m3") @ unpack4(c_words, c_scales)
    d = f64(susceptible) * force - f64(recovery) * x
    return (mxq(d, 1, "e5m2") @ mxq(f64(w), 0, "e4m3")) + f64(b)

@@ -1,0 +1,331 @@
+from contextlib import ExitStack
+
+import concourse.mybir as mybir
+from concourse.masks import make_identity
+
+M, H, R = 512, 2048, 1024
+FLOPS = 2 * M * H * H + 2 * M * H * R
+
+F32 = mybir.dt.float32
+BF16 = mybir.dt.bfloat16
+I32 = mybir.dt.int32
+U32 = mybir.dt.uint32
+U8 = mybir.dt.uint8
+E4M3 = mybir.dt.float8_e4m3fn_x4
+E5M2 = mybir.dt.float8_e5m2_x4
+E2M1 = mybir.dt.float4_e2m1fn_x4
+ALU = mybir.AluOpType
+COPY = mybir.ActivationFunctionType.Copy
+
+P = 128
+PACK = 4
+KP = P * PACK
+G = H // KP
+MT = M // P
+NB = 512
+RH = R // NB
+
+
+def tile_malware_outbreak_readout_s9_kernel(tc, x, c_words, c_scales, susceptible, recovery, w, b, out):
+    nc = tc.nc
+    with ExitStack() as ctx:
+        keep = ctx.enter_context(tc.tile_pool(name="keep", bufs=1))
+        work = ctx.enter_context(tc.tile_pool(name="work", bufs=3))
+        psum = ctx.enter_context(tc.psum_pool(name="psum", bufs=4))
+        ctx.enter_context(tc.manual_schedule())
+
+        def kept(name, shape, dtype):
+            return keep.tile(shape, dtype, name=name, align_bytes=64)
+
+        ident = kept("ident", [P, P], F32)
+        rec_raw = kept("rec_raw", [P, G, PACK], BF16)
+        rec = kept("rec", [P, G * PACK], F32)
+        bias = kept("bias", [P, R], BF16)
+        cs_first = kept("cs_first", [P, G, NB], U8)
+        cs_rest = kept("cs_rest", [P, G, H - NB], U8)
+        c_tiles = [kept("c_%d" % n, [P, G, 2 * NB], U8) for n in range(G)]
+        x0 = [kept("x0_%d" % h, [P, H // 2], BF16) for h in range(2)]
+        x_rest = [kept("x_%d" % mt, [P, H], BF16) for mt in range(1, MT)]
+        sus0 = [kept("sus0_%d" % h, [P, 2, NB], BF16) for h in range(2)]
+        sus_rest = [kept("sus_%d" % n, [P, MT, NB], BF16) for n in range(1, G)]
+        w_raw = [[kept("w_%d_%d" % (h, g), [P, PACK, NB], BF16) for g in range(G)] for h in range(RH)]
+        xt_first = kept("xt_first", [P, H], BF16)
+        xt_rest = kept("xt_rest", [P, MT - 1, H], BF16)
+        x_codes = [kept("xc_%d" % mt, [P, G * P], U32) for mt in range(MT)]
+        x_scales = [kept("xs_%d" % mt, [P, G * P], U8) for mt in range(MT)]
+        rx_first = kept("rx_first", [P, G, PACK, P], F32)
+        rx_rest = [kept("rx_%d" % n, [P, PACK, MT - 1, P], F32) for n in range(G)]
+        d_codes = kept("d_codes", [P, G, M], U32)
+        d_scales = kept("d_scales", [P, G, M], U8)
+        w_codes = [[kept("wc_%d_%d" % (h, g), [P, NB], U32) for g in range(G)] for h in range(RH)]
+        w_scales = [[kept("ws_%d_%d" % (h, g), [P, NB], U8) for g in range(G)] for h in range(RH)]
+
+        nc.vector.memset(cs_first[:].bitcast(I32), 0)
+        nc.vector.memset(cs_rest[:].bitcast(I32), 0)
+        make_identity(nc, ident[:])
+
+        scale_rows = c_scales.bitcast(I32).rearrange("g (q r) n -> r q g n", r=4)
+        c_view = c_words.bitcast(I32).rearrange("g p n -> p g n")
+        sus_view = susceptible.rearrange("(mt p) n -> p mt n", p=P)
+
+        def load_scales(queue, plane, c0, c1):
+            for r in range(4):
+                queue.dma_start(out=plane[r:P:32, :, :].bitcast(I32), in_=scale_rows[r, :, :, c0 // 4 : c1 // 4])
+
+        def load_c(n):
+            nc.sync.dma_start(out=c_tiles[n][:].bitcast(I32), in_=c_view[:, :, n * NB // 2 : (n + 1) * NB // 2])
+
+        def load_x(mt):
+            nc.sync.dma_start(out=x_rest[mt - 1][:], in_=x[mt * P : (mt + 1) * P, :])
+
+        def load_sus(n):
+            nc.sync.dma_start(out=sus_rest[n - 1][:], in_=sus_view[:, :, n * NB : (n + 1) * NB])
+
+        def load_w(h, g):
+            rows = w[g * KP : (g + 1) * KP, h * NB : (h + 1) * NB]
+            nc.sync.dma_start(out=w_raw[h][g][:], in_=rows.rearrange("(p t) c -> p t c", t=PACK))
+
+        nc.scalar.dma_start(out=rec_raw[:], in_=recovery.rearrange("(g p t) -> p g t", p=P, t=PACK))
+        load_scales(nc.scalar, cs_first, 0, NB)
+        for h in range(2):
+            nc.sync.dma_start(out=x0[h][:], in_=x[0:P, h * H // 2 : (h + 1) * H // 2])
+        load_c(0)
+        load_x(1)
+        nc.sync.dma_start(out=sus0[0][:], in_=sus_view[:, 0:2, 0:NB])
+        load_x(2)
+        load_x(3)
+        nc.sync.dma_start(out=sus0[1][:], in_=sus_view[:, 2:4, 0:NB])
+        load_scales(nc.sync, cs_rest, NB, H)
+        load_c(1)
+        load_sus(1)
+        load_w(0, 0)
+        load_w(0, 1)
+        load_c(2)
+        load_sus(2)
+        load_w(0, 2)
+        load_w(0, 3)
+        load_c(3)
+        load_sus(3)
+        for g in range(G):
+            load_w(1, g)
+        nc.sync.dma_start(out=bias[:], in_=b.partition_broadcast(P))
+
+        nc.scalar.activation(out=rec[:], in_=rec_raw[:].rearrange("p g t -> p (g t)"), func=COPY)
+
+        def xt_of(mt):
+            return xt_first[:] if mt == 0 else xt_rest[:, mt - 1, :]
+
+        turned_x = {}
+        force = {}
+        infected = {}
+        turned = {}
+        d_pair = {}
+        w_grouped = {}
+
+        def turn_x(mt, half):
+            src = x0[half][:] if mt == 0 else x_rest[mt - 1][:, half * H // 2 : (half + 1) * H // 2]
+            words = src.bitcast(F32)
+            bank = psum.tile([P, 2, 2, P], F32, name="turn", tag="turn")
+            for g in range(2):
+                for u in range(2):
+                    nc.tensor.transpose(bank[:, g, u, :], words[:, 256 * g + u : 256 * (g + 1) : 2], ident[:])
+            turned_x[mt, half] = bank
+
+        def empty_x(mt, half, on_vector):
+            dst = xt_of(mt)[:, half * H // 2 : (half + 1) * H // 2].bitcast(F32).rearrange("p (g m u) -> p g m u", g=2, u=2)
+            src = turned_x[mt, half][:].rearrange("p g u m -> p g m u")
+            if on_vector:
+                nc.vector.tensor_copy(out=dst, in_=src)
+            else:
+                nc.scalar.copy(out=dst, in_=src)
+
+        def quantize_x(mt, c0, c1):
+            nc.vector.quantize_mx(
+                out=x_codes[mt][:, c0 // PACK : c1 // PACK].bitcast(E4M3),
+                scales=x_scales[mt][:, c0 // PACK : c1 // PACK],
+                in_=xt_of(mt)[:, c0:c1],
+            )
+
+        def recover_first(n):
+            src = xt_first[:].rearrange("p (g m t) -> p g t m", g=G, t=PACK)
+            for t in range(PACK):
+                j = n * PACK + t
+                nc.scalar.activation(out=rx_first[:, n, t, :], in_=src[:, n, t, :], func=COPY, scale=rec[:, j : j + 1])
+
+        def recover_rest(n):
+            src = xt_rest[:].rearrange("p a (g m t) -> p g t a m", g=G, t=PACK)
+            for t in range(PACK):
+                j = n * PACK + t
+                nc.scalar.activation(out=rx_rest[n][:, t, :, :], in_=src[:, n, t, :, :], func=COPY, scale=rec[:, j : j + 1])
+
+        def multiply_force(unit, passes=range(G)):
+            n, mt = divmod(unit, MT)
+            if unit not in force:
+                force[unit] = psum.tile([P, NB], F32, name="acc", tag="acc")
+            for g in passes:
+                plane = cs_first[:, g, :] if n == 0 else cs_rest[:, g, (n - 1) * NB : n * NB]
+                nc.tensor.matmul_mx(
+                    out=force[unit][:],
+                    lhsT=x_codes[mt][:, g * P : (g + 1) * P].bitcast(E4M3),
+                    lhsT_scale=x_scales[mt][:, g * P : (g + 1) * P],
+                    rhs=c_tiles[n][:, g, :].bitcast(E2M1),
+                    rhs_scale=plane,
+                    start=(g == 0),
+                    stop=(g == G - 1),
+                )
+
+        def infect(unit):
+            n, mt = divmod(unit, MT)
+            sus = sus0[mt // 2][:, mt % 2, :] if n == 0 else sus_rest[n - 1][:, mt, :]
+            infected[unit] = work.tile([P, PACK, P], F32, name="infected", tag="infected", bufs=4)
+            nc.vector.tensor_tensor(
+                out=infected[unit][:],
+                in0=force[unit][:].rearrange("p (q t) -> p t q", t=PACK),
+                in1=sus.rearrange("p (q t) -> p t q", t=PACK),
+                op=ALU.mult,
+            )
+
+        def turn(unit):
+            turned[unit] = psum.tile([P, PACK, P], F32, name="turn", tag="turn")
+            for t in range(PACK):
+                nc.tensor.transpose(turned[unit][:, t, :], infected[unit][:, t, :], ident[:])
+
+        def subtract(unit):
+            n, mt = divmod(unit, MT)
+            if unit % 2 == 0:
+                d_pair[unit // 2] = work.tile([P, 2, P, PACK], BF16, name="d_pair", tag="d_pair", align_bytes=64)
+            rx = rx_first[:, n, :, :] if mt == 0 else rx_rest[n][:, :, mt - 1, :]
+            nc.vector.tensor_tensor(
+                out=d_pair[unit // 2][:, unit % 2, :, :],
+                in0=turned[unit][:].rearrange("p t m -> p m t"),
+                in1=rx.rearrange("p t m -> p m t"),
+                op=ALU.subtract,
+            )
+
+        def quantize_d(pair):
+            n, half = divmod(pair, 2)
+            cols = slice(half * 2 * P, (half + 1) * 2 * P)
+            nc.vector.quantize_mx(
+                out=d_codes[:, n, cols].bitcast(E5M2),
+                scales=d_scales[:, n, cols],
+                in_=d_pair[pair][:].rearrange("p a m t -> p (a m t)"),
+            )
+
+        def group_w(h, g, on_vector=False):
+            w_grouped[h, g] = work.tile([P, NB, PACK], BF16, name="w_grouped", tag="w_grouped", align_bytes=64)
+            dst = w_grouped[h, g][:].rearrange("p (c i) t -> p c t i", i=4)
+            src = w_raw[h][g][:].rearrange("p t (c i) -> p c t i", i=4)
+            if on_vector:
+                nc.vector.tensor_copy(out=dst, in_=src)
+            else:
+                nc.scalar.copy(out=dst, in_=src)
+
+        def quantize_w(h, g):
+            nc.vector.quantize_mx(
+                out=w_codes[h][g][:].bitcast(E4M3),
+                scales=w_scales[h][g][:],
+                in_=w_grouped[h, g][:].rearrange("p c t -> p (c t)"),
+            )
+
+        scores = {}
+
+        def multiply_out(h, mt):
+            scores[h, mt] = psum.tile([P, NB], F32, name="acc", tag="acc")
+            for g in range(G):
+                nc.tensor.matmul_mx(
+                    out=scores[h, mt][:],
+                    lhsT=d_codes[:, g, mt * P : (mt + 1) * P].bitcast(E5M2),
+                    lhsT_scale=d_scales[:, g, mt * P : (mt + 1) * P],
+                    rhs=w_codes[h][g][:].bitcast(E4M3),
+                    rhs_scale=w_scales[h][g][:],
+                    start=(g == 0),
+                    stop=(g == G - 1),
+                )
+
+        def store(h, mt):
+            cols = slice(h * NB, (h + 1) * NB)
+            result = work.tile([P, NB], F32, name="result", tag="result")
+            nc.vector.tensor_tensor(out=result[:], in0=scores[h, mt][:], in1=bias[:, cols], op=ALU.add)
+            nc.sync.dma_start(out=out[mt * P : (mt + 1) * P, cols], in_=result[:])
+
+        turn_x(0, 0)
+        turn_x(0, 1)
+        empty_x(0, 0, True)
+        empty_x(0, 1, False)
+        quantize_x(0, 0, H // 2)
+        quantize_x(0, H // 2, H)
+        for n in range(G):
+            recover_first(n)
+        multiply_force(0)
+        turn_x(1, 0)
+        turn_x(1, 1)
+        empty_x(1, 0, True)
+        empty_x(1, 1, True)
+        infect(0)
+        quantize_x(1, 0, H)
+        turn_x(2, 0)
+        turn_x(2, 1)
+        empty_x(2, 0, False)
+        empty_x(2, 1, False)
+        multiply_force(1)
+        turn_x(3, 0)
+        turn_x(3, 1)
+        empty_x(3, 0, False)
+        empty_x(3, 1, False)
+        quantize_x(2, 0, H)
+        infect(1)
+        quantize_x(3, 0, H)
+        recover_rest(0)
+        recover_rest(1)
+        multiply_force(2)
+        multiply_force(3)
+        turn(0)
+        turn(1)
+        scalar_work = {2: [(0, 0), 2], 3: [(0, 1)], 4: [(0, 2), 3], 5: [(0, 3)], 6: [(1, 0)], 7: [(1, 1)]}
+        w_ready = {4: [(0, 0)], 5: [(0, 1)], 6: [(0, 2)], 7: [(0, 3)]}
+        for j in range(2, 8):
+            infect(2 * j - 2)
+            if j >= 3:
+                quantize_d(j - 3)
+            for item in w_ready.get(j, []):
+                quantize_w(item[0], item[1])
+            for item in scalar_work.get(j, []):
+                if isinstance(item, int):
+                    recover_rest(item)
+                else:
+                    group_w(item[0], item[1])
+            infect(2 * j - 1)
+            subtract(2 * j - 4)
+            subtract(2 * j - 3)
+            multiply_force(2 * j)
+            multiply_force(2 * j + 1)
+            turn(2 * j - 2)
+            turn(2 * j - 1)
+        infect(14)
+        quantize_d(5)
+        infect(15)
+        subtract(12)
+        subtract(13)
+        turn(14)
+        turn(15)
+        quantize_w(1, 0)
+        group_w(1, 2)
+        quantize_d(6)
+        subtract(14)
+        subtract(15)
+        multiply_out(0, 0)
+        multiply_out(0, 1)
+        group_w(1, 3, True)
+        quantize_d(7)
+        store(0, 0)
+        quantize_w(1, 1)
+        multiply_out(0, 2)
+        multiply_out(0, 3)
+        store(0, 1)
+        quantize_w(1, 3)
+        quantize_w(1, 2)
+        store(0, 2)
+        store(0, 3)
+        for mt in range(MT):
+            multiply_out(1, mt)
+            store(1, mt)

@@ -24,6 +24,7 @@ G = H // KP
 MT = M // P
 NB = 512
 RH = R // NB
+HALF = H // 2
 
 
 def tile_malware_outbreak_readout_s9_kernel(tc, x, c_words, c_scales, susceptible, recovery, w, b, out):
@@ -41,36 +42,30 @@ def tile_malware_outbreak_readout_s9_kernel(tc, x, c_words, c_scales, susceptibl
         rec_raw = kept("rec_raw", [P, G, PACK], BF16)
         rec = kept("rec", [P, G * PACK], F32)
         bias = kept("bias", [P, R], BF16)
-        cs_first = kept("cs_first", [P, G, NB], U8)
-        cs_rest = kept("cs_rest", [P, G, H - NB], U8)
+        c_planes = [kept("cs_%d" % h, [P, G, HALF], U8) for h in range(2)]
         c_tiles = [kept("c_%d" % n, [P, G, 2 * NB], U8) for n in range(G)]
-        x0 = [kept("x0_%d" % h, [P, H // 2], BF16) for h in range(2)]
+        x_first = [kept("x0_%d" % h, [P, HALF], BF16) for h in range(2)]
         x_rest = [kept("x_%d" % mt, [P, H], BF16) for mt in range(1, MT)]
-        sus0 = [kept("sus0_%d" % h, [P, 2, NB], BF16) for h in range(2)]
-        sus_rest = [kept("sus_%d" % n, [P, MT, NB], BF16) for n in range(1, G)]
+        sus = [kept("sus_%d" % mt, [P, H], BF16) for mt in range(MT)]
         w_raw = [[kept("w_%d_%d" % (h, g), [P, PACK, NB], BF16) for g in range(G)] for h in range(RH)]
-        xt_first = kept("xt_first", [P, H], BF16)
-        xt_rest = kept("xt_rest", [P, MT - 1, H], BF16)
+        xt = [[kept("xt_%d_%d" % (mt, h), [P, HALF], BF16) for h in range(2)] for mt in range(MT)]
         x_codes = [kept("xc_%d" % mt, [P, G * P], U32) for mt in range(MT)]
         x_scales = [kept("xs_%d" % mt, [P, G * P], U8) for mt in range(MT)]
-        rx_first = kept("rx_first", [P, G, PACK, P], F32)
-        rx_rest = [kept("rx_%d" % n, [P, PACK, MT - 1, P], F32) for n in range(G)]
-        d_codes = kept("d_codes", [P, G, M], U32)
-        d_scales = kept("d_scales", [P, G, M], U8)
+        d_codes = [kept("dc_%d" % mt, [P, G * P], U32) for mt in range(MT)]
+        d_scales = [kept("ds_%d" % mt, [P, G * P], U8) for mt in range(MT)]
         w_codes = [[kept("wc_%d_%d" % (h, g), [P, NB], U32) for g in range(G)] for h in range(RH)]
         w_scales = [[kept("ws_%d_%d" % (h, g), [P, NB], U8) for g in range(G)] for h in range(RH)]
 
-        nc.vector.memset(cs_first[:].bitcast(I32), 0)
-        nc.vector.memset(cs_rest[:].bitcast(I32), 0)
+        for h in range(2):
+            nc.vector.memset(c_planes[h][:].bitcast(I32), 0)
         make_identity(nc, ident[:])
 
         scale_rows = c_scales.bitcast(I32).rearrange("g (q r) n -> r q g n", r=4)
         c_view = c_words.bitcast(I32).rearrange("g p n -> p g n")
-        sus_view = susceptible.rearrange("(mt p) n -> p mt n", p=P)
 
-        def load_scales(queue, plane, c0, c1):
+        def load_scales(queue, h):
             for r in range(4):
-                queue.dma_start(out=plane[r:P:32, :, :].bitcast(I32), in_=scale_rows[r, :, :, c0 // 4 : c1 // 4])
+                queue.dma_start(out=c_planes[h][r:P:32, :, :].bitcast(I32), in_=scale_rows[r, :, :, h * HALF // 4 : (h + 1) * HALF // 4])
 
         def load_c(n):
             nc.sync.dma_start(out=c_tiles[n][:].bitcast(I32), in_=c_view[:, :, n * NB // 2 : (n + 1) * NB // 2])
@@ -78,52 +73,55 @@ def tile_malware_outbreak_readout_s9_kernel(tc, x, c_words, c_scales, susceptibl
         def load_x(mt):
             nc.sync.dma_start(out=x_rest[mt - 1][:], in_=x[mt * P : (mt + 1) * P, :])
 
-        def load_sus(n):
-            nc.sync.dma_start(out=sus_rest[n - 1][:], in_=sus_view[:, :, n * NB : (n + 1) * NB])
+        def load_sus(mt, c0=0, c1=H):
+            nc.sync.dma_start(out=sus[mt][:, c0:c1], in_=susceptible[mt * P : (mt + 1) * P, c0:c1])
 
         def load_w(h, g):
             rows = w[g * KP : (g + 1) * KP, h * NB : (h + 1) * NB]
             nc.sync.dma_start(out=w_raw[h][g][:], in_=rows.rearrange("(p t) c -> p t c", t=PACK))
 
-        nc.scalar.dma_start(out=rec_raw[:], in_=recovery.rearrange("(g p t) -> p g t", p=P, t=PACK))
-        load_scales(nc.scalar, cs_first, 0, NB)
+        nc.gpsimd.dma_start(out=rec_raw[:], in_=recovery.rearrange("(g p t) -> p g t", p=P, t=PACK))
         for h in range(2):
-            nc.sync.dma_start(out=x0[h][:], in_=x[0:P, h * H // 2 : (h + 1) * H // 2])
-        load_c(0)
+            nc.sync.dma_start(out=x_first[h][:], in_=x[0:P, h * HALF : (h + 1) * HALF])
         load_x(1)
-        nc.sync.dma_start(out=sus0[0][:], in_=sus_view[:, 0:2, 0:NB])
-        load_x(2)
-        load_x(3)
-        nc.sync.dma_start(out=sus0[1][:], in_=sus_view[:, 2:4, 0:NB])
-        load_scales(nc.sync, cs_rest, NB, H)
+        load_scales(nc.sync, 0)
+        load_c(0)
         load_c(1)
-        load_sus(1)
+        load_sus(0, 0, HALF)
+        load_sus(1, 0, HALF)
         load_w(0, 0)
-        load_w(0, 1)
+        load_scales(nc.sync, 1)
         load_c(2)
-        load_sus(2)
-        load_w(0, 2)
-        load_w(0, 3)
+        load_w(0, 1)
         load_c(3)
+        load_sus(0, HALF, H)
+        load_x(2)
+        load_sus(1, HALF, H)
+        load_w(0, 2)
+        load_sus(2)
+        load_x(3)
+        load_w(0, 3)
+        load_w(1, 0)
         load_sus(3)
-        for g in range(G):
-            load_w(1, g)
+        load_w(1, 1)
+        load_w(1, 2)
+        load_w(1, 3)
         nc.sync.dma_start(out=bias[:], in_=b.partition_broadcast(P))
 
         nc.scalar.activation(out=rec[:], in_=rec_raw[:].rearrange("p g t -> p (g t)"), func=COPY)
 
-        def xt_of(mt):
-            return xt_first[:] if mt == 0 else xt_rest[:, mt - 1, :]
-
+        order = [(0, 0), (1, 0), (0, 1), (1, 1), (2, 0), (2, 1), (3, 0), (3, 1)]
         turned_x = {}
+        recovered = {}
         force = {}
         infected = {}
         turned = {}
         d_pair = {}
         w_grouped = {}
+        scores = {}
 
         def turn_x(mt, half):
-            src = x0[half][:] if mt == 0 else x_rest[mt - 1][:, half * H // 2 : (half + 1) * H // 2]
+            src = x_first[half][:] if mt == 0 else x_rest[mt - 1][:, half * HALF : (half + 1) * HALF]
             words = src.bitcast(F32)
             bank = psum.tile([P, 2, 2, P], F32, name="turn", tag="turn")
             for g in range(2):
@@ -131,57 +129,48 @@ def tile_malware_outbreak_readout_s9_kernel(tc, x, c_words, c_scales, susceptibl
                     nc.tensor.transpose(bank[:, g, u, :], words[:, 256 * g + u : 256 * (g + 1) : 2], ident[:])
             turned_x[mt, half] = bank
 
-        def empty_x(mt, half, on_vector):
-            dst = xt_of(mt)[:, half * H // 2 : (half + 1) * H // 2].bitcast(F32).rearrange("p (g m u) -> p g m u", g=2, u=2)
+        def empty_x(mt, half, on_vector=False):
+            dst = xt[mt][half][:].bitcast(F32).rearrange("p (g m u) -> p g m u", g=2, u=2)
             src = turned_x[mt, half][:].rearrange("p g u m -> p g m u")
             if on_vector:
                 nc.vector.tensor_copy(out=dst, in_=src)
             else:
                 nc.scalar.copy(out=dst, in_=src)
 
-        def quantize_x(mt, c0, c1):
-            nc.vector.quantize_mx(
-                out=x_codes[mt][:, c0 // PACK : c1 // PACK].bitcast(E4M3),
-                scales=x_scales[mt][:, c0 // PACK : c1 // PACK],
-                in_=xt_of(mt)[:, c0:c1],
-            )
+        def quantize_x(mt, half):
+            cols = slice(half * 2 * P, (half + 1) * 2 * P)
+            nc.vector.quantize_mx(out=x_codes[mt][:, cols].bitcast(E4M3), scales=x_scales[mt][:, cols], in_=xt[mt][half][:])
 
-        def recover_first(n):
-            src = xt_first[:].rearrange("p (g m t) -> p g t m", g=G, t=PACK)
-            for t in range(PACK):
-                j = n * PACK + t
-                nc.scalar.activation(out=rx_first[:, n, t, :], in_=src[:, n, t, :], func=COPY, scale=rec[:, j : j + 1])
+        def recover(pair):
+            mt, half = order[pair]
+            recovered[pair] = work.tile([P, 2, PACK, P], F32, name="recovered", tag="recovered", bufs=4)
+            src = xt[mt][half][:].rearrange("p (g m t) -> p g t m", g=2, t=PACK)
+            for g in range(2):
+                for t in range(PACK):
+                    j = (2 * half + g) * PACK + t
+                    nc.scalar.activation(out=recovered[pair][:, g, t, :], in_=src[:, g, t, :], func=COPY, scale=rec[:, j : j + 1])
 
-        def recover_rest(n):
-            src = xt_rest[:].rearrange("p a (g m t) -> p g t a m", g=G, t=PACK)
-            for t in range(PACK):
-                j = n * PACK + t
-                nc.scalar.activation(out=rx_rest[n][:, t, :, :], in_=src[:, n, t, :, :], func=COPY, scale=rec[:, j : j + 1])
-
-        def multiply_force(unit, passes=range(G)):
-            n, mt = divmod(unit, MT)
-            if unit not in force:
-                force[unit] = psum.tile([P, NB], F32, name="acc", tag="acc")
-            for g in passes:
-                plane = cs_first[:, g, :] if n == 0 else cs_rest[:, g, (n - 1) * NB : n * NB]
+        def multiply_force(unit):
+            mt, n = order[unit // 2][0], 2 * order[unit // 2][1] + unit % 2
+            force[unit] = psum.tile([P, NB], F32, name="acc", tag="acc")
+            for g in range(G):
                 nc.tensor.matmul_mx(
                     out=force[unit][:],
                     lhsT=x_codes[mt][:, g * P : (g + 1) * P].bitcast(E4M3),
                     lhsT_scale=x_scales[mt][:, g * P : (g + 1) * P],
                     rhs=c_tiles[n][:, g, :].bitcast(E2M1),
-                    rhs_scale=plane,
+                    rhs_scale=c_planes[n // 2][:, g, (n % 2) * NB : (n % 2 + 1) * NB],
                     start=(g == 0),
                     stop=(g == G - 1),
                 )
 
         def infect(unit):
-            n, mt = divmod(unit, MT)
-            sus = sus0[mt // 2][:, mt % 2, :] if n == 0 else sus_rest[n - 1][:, mt, :]
+            mt, n = order[unit // 2][0], 2 * order[unit // 2][1] + unit % 2
             infected[unit] = work.tile([P, PACK, P], F32, name="infected", tag="infected", bufs=4)
             nc.vector.tensor_tensor(
                 out=infected[unit][:],
                 in0=force[unit][:].rearrange("p (q t) -> p t q", t=PACK),
-                in1=sus.rearrange("p (q t) -> p t q", t=PACK),
+                in1=sus[mt][:, n * NB : (n + 1) * NB].rearrange("p (q t) -> p t q", t=PACK),
                 op=ALU.mult,
             )
 
@@ -191,34 +180,31 @@ def tile_malware_outbreak_readout_s9_kernel(tc, x, c_words, c_scales, susceptibl
                 nc.tensor.transpose(turned[unit][:, t, :], infected[unit][:, t, :], ident[:])
 
         def subtract(unit):
-            n, mt = divmod(unit, MT)
-            if unit % 2 == 0:
-                d_pair[unit // 2] = work.tile([P, 2, P, PACK], BF16, name="d_pair", tag="d_pair", align_bytes=64)
-            rx = rx_first[:, n, :, :] if mt == 0 else rx_rest[n][:, :, mt - 1, :]
+            pair, g = divmod(unit, 2)
+            if g == 0:
+                d_pair[pair] = work.tile([P, 2, P, PACK], BF16, name="d_pair", tag="d_pair", align_bytes=64)
             nc.vector.tensor_tensor(
-                out=d_pair[unit // 2][:, unit % 2, :, :],
-                in0=turned[unit][:].rearrange("p t m -> p m t"),
-                in1=rx.rearrange("p t m -> p m t"),
+                out=d_pair[pair][:, g, :, :].rearrange("p (a i) t -> p a t i", i=2),
+                in0=turned[unit][:].rearrange("p t (a i) -> p a t i", i=2),
+                in1=recovered[pair][:, g, :, :].rearrange("p t (a i) -> p a t i", i=2),
                 op=ALU.subtract,
             )
 
         def quantize_d(pair):
-            n, half = divmod(pair, 2)
+            mt, half = order[pair]
             cols = slice(half * 2 * P, (half + 1) * 2 * P)
             nc.vector.quantize_mx(
-                out=d_codes[:, n, cols].bitcast(E5M2),
-                scales=d_scales[:, n, cols],
+                out=d_codes[mt][:, cols].bitcast(E5M2),
+                scales=d_scales[mt][:, cols],
                 in_=d_pair[pair][:].rearrange("p a m t -> p (a m t)"),
             )
 
-        def group_w(h, g, on_vector=False):
-            w_grouped[h, g] = work.tile([P, NB, PACK], BF16, name="w_grouped", tag="w_grouped", align_bytes=64)
-            dst = w_grouped[h, g][:].rearrange("p (c i) t -> p c t i", i=4)
-            src = w_raw[h][g][:].rearrange("p t (c i) -> p c t i", i=4)
-            if on_vector:
-                nc.vector.tensor_copy(out=dst, in_=src)
-            else:
-                nc.scalar.copy(out=dst, in_=src)
+        def group_w(h, g):
+            w_grouped[h, g] = work.tile([P, NB, PACK], BF16, name="w_grouped", tag="w_grouped", align_bytes=64, bufs=4)
+            nc.scalar.copy(
+                out=w_grouped[h, g][:].rearrange("p (c i) t -> p c t i", i=4),
+                in_=w_raw[h][g][:].rearrange("p t (c i) -> p c t i", i=4),
+            )
 
         def quantize_w(h, g):
             nc.vector.quantize_mx(
@@ -227,15 +213,14 @@ def tile_malware_outbreak_readout_s9_kernel(tc, x, c_words, c_scales, susceptibl
                 in_=w_grouped[h, g][:].rearrange("p c t -> p (c t)"),
             )
 
-        scores = {}
-
         def multiply_out(h, mt):
-            scores[h, mt] = psum.tile([P, NB], F32, name="acc", tag="acc")
+            tag = "acc" if h == 0 else "turn"
+            scores[h, mt] = psum.tile([P, NB], F32, name=tag, tag=tag)
             for g in range(G):
                 nc.tensor.matmul_mx(
                     out=scores[h, mt][:],
-                    lhsT=d_codes[:, g, mt * P : (mt + 1) * P].bitcast(E5M2),
-                    lhsT_scale=d_scales[:, g, mt * P : (mt + 1) * P],
+                    lhsT=d_codes[mt][:, g * P : (g + 1) * P].bitcast(E5M2),
+                    lhsT_scale=d_scales[mt][:, g * P : (g + 1) * P],
                     rhs=w_codes[h][g][:].bitcast(E4M3),
                     rhs_scale=w_scales[h][g][:],
                     start=(g == 0),
@@ -244,88 +229,83 @@ def tile_malware_outbreak_readout_s9_kernel(tc, x, c_words, c_scales, susceptibl
 
         def store(h, mt):
             cols = slice(h * NB, (h + 1) * NB)
-            result = work.tile([P, NB], F32, name="result", tag="result")
+            result = work.tile([P, NB], F32, name="result", tag="result", bufs=8)
             nc.vector.tensor_tensor(out=result[:], in0=scores[h, mt][:], in1=bias[:, cols], op=ALU.add)
             nc.sync.dma_start(out=out[mt * P : (mt + 1) * P, cols], in_=result[:])
 
+        w_parts = [(h, g) for h in range(RH) for g in range(G)]
+        pairs = 2 * MT
         turn_x(0, 0)
         turn_x(0, 1)
         empty_x(0, 0, True)
-        empty_x(0, 1, False)
-        quantize_x(0, 0, H // 2)
-        quantize_x(0, H // 2, H)
-        for n in range(G):
-            recover_first(n)
-        multiply_force(0)
+        empty_x(0, 1)
+        quantize_x(0, 0)
+        quantize_x(0, 1)
+        recover(0)
+
         turn_x(1, 0)
         turn_x(1, 1)
         empty_x(1, 0, True)
-        empty_x(1, 1, True)
-        infect(0)
-        quantize_x(1, 0, H)
-        turn_x(2, 0)
-        turn_x(2, 1)
-        empty_x(2, 0, False)
-        empty_x(2, 1, False)
-        multiply_force(1)
-        turn_x(3, 0)
-        turn_x(3, 1)
-        empty_x(3, 0, False)
-        empty_x(3, 1, False)
-        quantize_x(2, 0, H)
-        infect(1)
-        quantize_x(3, 0, H)
-        recover_rest(0)
-        recover_rest(1)
-        multiply_force(2)
-        multiply_force(3)
-        turn(0)
-        turn(1)
-        scalar_work = {2: [(0, 0), 2], 3: [(0, 1)], 4: [(0, 2), 3], 5: [(0, 3)], 6: [(1, 0)], 7: [(1, 1)]}
-        w_ready = {4: [(0, 0)], 5: [(0, 1)], 6: [(0, 2)], 7: [(0, 3)]}
-        for j in range(2, 8):
-            infect(2 * j - 2)
-            if j >= 3:
-                quantize_d(j - 3)
-            for item in w_ready.get(j, []):
-                quantize_w(item[0], item[1])
-            for item in scalar_work.get(j, []):
-                if isinstance(item, int):
-                    recover_rest(item)
-                else:
-                    group_w(item[0], item[1])
-            infect(2 * j - 1)
-            subtract(2 * j - 4)
-            subtract(2 * j - 3)
-            multiply_force(2 * j)
+        empty_x(1, 1)
+        quantize_x(1, 0)
+        quantize_x(1, 1)
+        recover(1)
+        recover(2)
+        multiply_force(0)
+        scalar_work = ["w0 r3", "w1", "e r4", "w2 r5", "w3 e", "r6 w4", "r7 w5", "w6"]
+        w_ready = [[], [], [0], [1], [], [2], [3], [], [4], [5, 6]]
+        for j in range(pairs):
+            next_x = {2: 2, 4: 3}.get(j)
+            if j > 0:
+                multiply_force(2 * j)
             multiply_force(2 * j + 1)
-            turn(2 * j - 2)
-            turn(2 * j - 1)
-        infect(14)
-        quantize_d(5)
-        infect(15)
-        subtract(12)
-        subtract(13)
-        turn(14)
-        turn(15)
-        quantize_w(1, 0)
-        group_w(1, 2)
-        quantize_d(6)
-        subtract(14)
-        subtract(15)
+            if j >= 1:
+                turn(2 * j - 2)
+                turn(2 * j - 1)
+            if next_x:
+                turn_x(next_x, 0)
+                turn_x(next_x, 1)
+            infect(2 * j)
+            if j in (3, 5):
+                quantize_x(j // 2 + 1, 0)
+                quantize_x(j // 2 + 1, 1)
+            if j >= 2:
+                quantize_d(j - 2)
+            for k in w_ready[j]:
+                quantize_w(*w_parts[k])
+            infect(2 * j + 1)
+            if j >= 1:
+                subtract(2 * j - 2)
+                subtract(2 * j - 1)
+            for item in scalar_work[j].split():
+                if item[0] == "w":
+                    group_w(*w_parts[int(item[1])])
+                elif item[0] == "r":
+                    recover(int(item[1]))
+                else:
+                    empty_x(next_x, 0)
+                    empty_x(next_x, 1)
         multiply_out(0, 0)
         multiply_out(0, 1)
-        group_w(1, 3, True)
-        quantize_d(7)
+        turn(2 * pairs - 2)
+        turn(2 * pairs - 1)
+        quantize_d(pairs - 2)
+        for k in w_ready[8]:
+            quantize_w(*w_parts[k])
+        group_w(*w_parts[7])
+        subtract(2 * pairs - 2)
+        subtract(2 * pairs - 1)
         store(0, 0)
-        quantize_w(1, 1)
+        quantize_d(pairs - 1)
         multiply_out(0, 2)
         multiply_out(0, 3)
+        for k in w_ready[9]:
+            quantize_w(*w_parts[k])
         store(0, 1)
-        quantize_w(1, 3)
-        quantize_w(1, 2)
-        store(0, 2)
-        store(0, 3)
+        quantize_w(*w_parts[7])
         for mt in range(MT):
             multiply_out(1, mt)
+        for mt in range(2, MT):
+            store(0, mt)
+        for mt in range(MT):
             store(1, mt)

@@ -80,9 +80,9 @@ def tile_malware_outbreak_readout_s9_kernel(tc, x, c_words, c_scales, susceptibl
             rows = w[g * KP : (g + 1) * KP, h * NB : (h + 1) * NB]
             nc.sync.dma_start(out=w_raw[h][g][:], in_=rows.rearrange("(p t) c -> p t c", t=PACK))
 
-        nc.gpsimd.dma_start(out=rec_raw[:], in_=recovery.rearrange("(g p t) -> p g t", p=P, t=PACK))
         for h in range(2):
             nc.sync.dma_start(out=x_first[h][:], in_=x[0:P, h * HALF : (h + 1) * HALF])
+        nc.sync.dma_start(out=rec_raw[:], in_=recovery.rearrange("(g p t) -> p g t", p=P, t=PACK))
         load_x(1)
         load_scales(nc.sync, 0)
         load_c(0)
@@ -168,9 +168,9 @@ def tile_malware_outbreak_readout_s9_kernel(tc, x, c_words, c_scales, susceptibl
             mt, n = order[unit // 2][0], 2 * order[unit // 2][1] + unit % 2
             infected[unit] = work.tile([P, PACK, P], F32, name="infected", tag="infected", bufs=4)
             nc.vector.tensor_tensor(
-                out=infected[unit][:],
-                in0=force[unit][:].rearrange("p (q t) -> p t q", t=PACK),
-                in1=sus[mt][:, n * NB : (n + 1) * NB].rearrange("p (q t) -> p t q", t=PACK),
+                out=infected[unit][:].rearrange("p t (a i) -> p a t i", i=2),
+                in0=force[unit][:].rearrange("p (a i t) -> p a t i", i=2, t=PACK),
+                in1=sus[mt][:, n * NB : (n + 1) * NB].rearrange("p (a i t) -> p a t i", i=2, t=PACK),
                 op=ALU.mult,
             )
 
@@ -227,11 +227,13 @@ def tile_malware_outbreak_readout_s9_kernel(tc, x, c_words, c_scales, susceptibl
                     stop=(g == G - 1),
                 )
 
-        def store(h, mt):
-            cols = slice(h * NB, (h + 1) * NB)
-            result = work.tile([P, NB], F32, name="result", tag="result", bufs=8)
-            nc.vector.tensor_tensor(out=result[:], in0=scores[h, mt][:], in1=bias[:, cols], op=ALU.add)
-            nc.sync.dma_start(out=out[mt * P : (mt + 1) * P, cols], in_=result[:])
+        def store(h, mt, pieces=1):
+            width = NB // pieces
+            for c in range(0, NB, width):
+                cols = slice(h * NB + c, h * NB + c + width)
+                result = work.tile([P, width], F32, name="result", tag="result", bufs=9)
+                nc.vector.tensor_tensor(out=result[:], in0=scores[h, mt][:, c : c + width], in1=bias[:, cols], op=ALU.add)
+                nc.sync.dma_start(out=out[mt * P : (mt + 1) * P, cols], in_=result[:])
 
         w_parts = [(h, g) for h in range(RH) for g in range(G)]
         pairs = 2 * MT
@@ -253,7 +255,7 @@ def tile_malware_outbreak_readout_s9_kernel(tc, x, c_words, c_scales, susceptibl
         recover(2)
         multiply_force(0)
         scalar_work = ["w0 r3", "w1", "e r4", "w2 r5", "w3 e", "r6 w4", "r7 w5", "w6"]
-        w_ready = [[], [], [0], [1], [], [2], [3], [], [4], [5, 6]]
+        w_ready = [[], [], [0], [1], [2], [], [3], [], [4], [5, 6]]
         for j in range(pairs):
             next_x = {2: 2, 4: 3}.get(j)
             if j > 0:
@@ -308,4 +310,4 @@ def tile_malware_outbreak_readout_s9_kernel(tc, x, c_words, c_scales, susceptibl
         for mt in range(2, MT):
             store(0, mt)
         for mt in range(MT):
-            store(1, mt)
+            store(1, mt, 2 if mt == MT - 1 else 1)

@@ -32,87 +32,80 @@ def tile_malware_outbreak_readout_s9_kernel(tc, x, c_words, c_scales, susceptibl
     with ExitStack() as ctx:
         keep = ctx.enter_context(tc.tile_pool(name="keep", bufs=1))
         work = ctx.enter_context(tc.tile_pool(name="work", bufs=3))
-        psum = ctx.enter_context(tc.psum_pool(name="psum", bufs=4))
+        psum = ctx.enter_context(tc.psum_pool(name="psum", bufs=8))
         ctx.enter_context(tc.manual_schedule())
 
         def kept(name, shape, dtype):
             return keep.tile(shape, dtype, name=name, align_bytes=64)
 
         ident = kept("ident", [P, P], F32)
-        rec_raw = kept("rec_raw", [P, G, PACK], BF16)
+        rec_raw = kept("rec_raw", [P, G * PACK], BF16)
         rec = kept("rec", [P, G * PACK], F32)
         bias = kept("bias", [P, R], BF16)
-        c_planes = [kept("cs_%d" % h, [P, G, HALF], U8) for h in range(2)]
-        c_tiles = [kept("c_%d" % n, [P, G, 2 * NB], U8) for n in range(G)]
+        c_codes = {(nh, gh): kept("c_%d_%d" % (nh, gh), [P, 2, 2 * HALF], U8) for nh in range(2) for gh in range(2)}
+        c_planes = {(nh, gh): kept("cs_%d_%d" % (nh, gh), [P, 2, HALF], U8) for nh in range(2) for gh in range(2)}
         x_first = [kept("x0_%d" % h, [P, HALF], BF16) for h in range(2)]
         x_rest = [kept("x_%d" % mt, [P, H], BF16) for mt in range(1, MT)]
-        sus = [kept("sus_%d" % mt, [P, H], BF16) for mt in range(MT)]
-        w_raw = [[kept("w_%d_%d" % (h, g), [P, PACK, NB], BF16) for g in range(G)] for h in range(RH)]
+        sus = {(mp, nh): kept("sus_%d_%d" % (mp, nh), [P, 2, HALF], BF16) for nh in range(2) for mp in range(2)}
+        w_raw = [kept("w_%d" % g, [P, PACK, R], BF16) for g in range(G)]
         xt = [[kept("xt_%d_%d" % (mt, h), [P, HALF], BF16) for h in range(2)] for mt in range(MT)]
+        recovered = [[kept("rx_%d_%d" % (mt, h), [P, 2, PACK, P], F32) for h in range(2)] for mt in range(MT)]
         x_codes = [kept("xc_%d" % mt, [P, G * P], U32) for mt in range(MT)]
         x_scales = [kept("xs_%d" % mt, [P, G * P], U8) for mt in range(MT)]
         d_codes = [kept("dc_%d" % mt, [P, G * P], U32) for mt in range(MT)]
         d_scales = [kept("ds_%d" % mt, [P, G * P], U8) for mt in range(MT)]
-        w_codes = [[kept("wc_%d_%d" % (h, g), [P, NB], U32) for g in range(G)] for h in range(RH)]
-        w_scales = [[kept("ws_%d_%d" % (h, g), [P, NB], U8) for g in range(G)] for h in range(RH)]
+        w_codes = {(h, g): kept("wc_%d_%d" % (h, g), [P, NB], U32) for h in range(RH) for g in range(G)}
+        w_scales = {(h, g): kept("ws_%d_%d" % (h, g), [P, NB], U8) for h in range(RH) for g in range(G)}
 
-        for h in range(2):
-            nc.vector.memset(c_planes[h][:].bitcast(I32), 0)
+        for plane in c_planes.values():
+            nc.vector.memset(plane[:].bitcast(I32), 0)
         make_identity(nc, ident[:])
 
         scale_rows = c_scales.bitcast(I32).rearrange("g (q r) n -> r q g n", r=4)
         c_view = c_words.bitcast(I32).rearrange("g p n -> p g n")
 
-        def load_scales(queue, h):
+        def load_c(nh, gh):
+            gs = slice(2 * gh, 2 * gh + 2)
             for r in range(4):
-                queue.dma_start(out=c_planes[h][r:P:32, :, :].bitcast(I32), in_=scale_rows[r, :, :, h * HALF // 4 : (h + 1) * HALF // 4])
-
-        def load_c(n):
-            nc.sync.dma_start(out=c_tiles[n][:].bitcast(I32), in_=c_view[:, :, n * NB // 2 : (n + 1) * NB // 2])
+                nc.sync.dma_start(
+                    out=c_planes[nh, gh][r:P:32, :, :].bitcast(I32),
+                    in_=scale_rows[r, :, gs, nh * HALF // 4 : (nh + 1) * HALF // 4],
+                )
+            nc.sync.dma_start(out=c_codes[nh, gh][:].bitcast(I32), in_=c_view[:, gs, nh * HALF // 2 : (nh + 1) * HALF // 2])
 
         def load_x(mt):
             nc.sync.dma_start(out=x_rest[mt - 1][:], in_=x[mt * P : (mt + 1) * P, :])
 
-        def load_sus(mt, c0=0, c1=H):
-            nc.sync.dma_start(out=sus[mt][:, c0:c1], in_=susceptible[mt * P : (mt + 1) * P, c0:c1])
+        def load_sus(mp, nh):
+            rows = susceptible[2 * mp * P : 2 * (mp + 1) * P, nh * HALF : (nh + 1) * HALF]
+            nc.sync.dma_start(out=sus[mp, nh][:], in_=rows.rearrange("(a p) c -> p a c", p=P))
 
-        def load_w(h, g):
-            rows = w[g * KP : (g + 1) * KP, h * NB : (h + 1) * NB]
-            nc.sync.dma_start(out=w_raw[h][g][:], in_=rows.rearrange("(p t) c -> p t c", t=PACK))
+        def load_w(g):
+            nc.sync.dma_start(out=w_raw[g][:], in_=w[g * KP : (g + 1) * KP, :].rearrange("(p t) c -> p t c", t=PACK))
 
         for h in range(2):
             nc.sync.dma_start(out=x_first[h][:], in_=x[0:P, h * HALF : (h + 1) * HALF])
-        nc.sync.dma_start(out=rec_raw[:], in_=recovery.rearrange("(g p t) -> p g t", p=P, t=PACK))
+        nc.sync.dma_start(out=rec_raw[:].rearrange("p (g t) -> p g t", t=PACK), in_=recovery.rearrange("(g p t) -> p g t", p=P, t=PACK))
+        load_c(0, 0)
         load_x(1)
-        load_scales(nc.sync, 0)
-        load_c(0)
-        load_c(1)
-        load_sus(0, 0, HALF)
-        load_sus(1, 0, HALF)
-        load_w(0, 0)
-        load_scales(nc.sync, 1)
-        load_c(2)
-        load_w(0, 1)
-        load_c(3)
-        load_sus(0, HALF, H)
+        load_c(0, 1)
         load_x(2)
-        load_sus(1, HALF, H)
-        load_w(0, 2)
-        load_sus(2)
+        load_sus(0, 0)
         load_x(3)
-        load_w(0, 3)
-        load_w(1, 0)
-        load_sus(3)
-        load_w(1, 1)
-        load_w(1, 2)
-        load_w(1, 3)
+        load_w(0)
+        load_sus(1, 0)
+        load_c(1, 0)
+        load_c(1, 1)
+        load_w(1)
+        load_sus(0, 1)
+        load_w(2)
+        load_w(3)
+        load_sus(1, 1)
         nc.sync.dma_start(out=bias[:], in_=b.partition_broadcast(P))
 
-        nc.scalar.activation(out=rec[:], in_=rec_raw[:].rearrange("p g t -> p (g t)"), func=COPY)
+        nc.scalar.activation(out=rec[:], in_=rec_raw[:], func=COPY)
 
-        order = [(0, 0), (1, 0), (0, 1), (1, 1), (2, 0), (2, 1), (3, 0), (3, 1)]
         turned_x = {}
-        recovered = {}
         force = {}
         infected = {}
         turned = {}
@@ -120,109 +113,115 @@ def tile_malware_outbreak_readout_s9_kernel(tc, x, c_words, c_scales, susceptibl
         w_grouped = {}
         scores = {}
 
-        def turn_x(mt, half):
-            src = x_first[half][:] if mt == 0 else x_rest[mt - 1][:, half * HALF : (half + 1) * HALF]
-            words = src.bitcast(F32)
-            bank = psum.tile([P, 2, 2, P], F32, name="turn", tag="turn")
-            for g in range(2):
-                for u in range(2):
-                    nc.tensor.transpose(bank[:, g, u, :], words[:, 256 * g + u : 256 * (g + 1) : 2], ident[:])
-            turned_x[mt, half] = bank
+        def bank(shape):
+            return psum.tile(shape, F32, name="bank", tag="bank")
 
-        def empty_x(mt, half, on_vector=False):
-            dst = xt[mt][half][:].bitcast(F32).rearrange("p (g m u) -> p g m u", g=2, u=2)
-            src = turned_x[mt, half][:].rearrange("p g u m -> p g m u")
-            if on_vector:
-                nc.vector.tensor_copy(out=dst, in_=src)
-            else:
-                nc.scalar.copy(out=dst, in_=src)
+        def place(unit):
+            pair, j = divmod(unit, 2)
+            nh, mt = divmod(pair, MT)
+            return mt, nh, j
+
+        def turn_x(mt):
+            for half in range(2):
+                src = x_first[half][:] if mt == 0 else x_rest[mt - 1][:, half * HALF : (half + 1) * HALF]
+                words = src.bitcast(F32)
+                turned_x[mt, half] = bank([P, 2, 2, P])
+                for g in range(2):
+                    for u in range(2):
+                        nc.tensor.transpose(turned_x[mt, half][:, g, u, :], words[:, 256 * g + u : 256 * (g + 1) : 2], ident[:])
+
+        def empty_x(mt, half, copy):
+            copy(
+                out=xt[mt][half][:].bitcast(F32).rearrange("p (g m u) -> p g m u", g=2, u=2),
+                in_=turned_x[mt, half][:].rearrange("p g u m -> p g m u"),
+            )
 
         def quantize_x(mt, half):
             cols = slice(half * 2 * P, (half + 1) * 2 * P)
             nc.vector.quantize_mx(out=x_codes[mt][:, cols].bitcast(E4M3), scales=x_scales[mt][:, cols], in_=xt[mt][half][:])
 
-        def recover(pair):
-            mt, half = order[pair]
-            recovered[pair] = work.tile([P, 2, PACK, P], F32, name="recovered", tag="recovered", bufs=4)
+        def recover(mt, half):
             src = xt[mt][half][:].rearrange("p (g m t) -> p g t m", g=2, t=PACK)
             for g in range(2):
                 for t in range(PACK):
                     j = (2 * half + g) * PACK + t
-                    nc.scalar.activation(out=recovered[pair][:, g, t, :], in_=src[:, g, t, :], func=COPY, scale=rec[:, j : j + 1])
+                    nc.scalar.activation(out=recovered[mt][half][:, g, t, :], in_=src[:, g, t, :], func=COPY, scale=rec[:, j : j + 1])
 
-        def multiply_force(unit):
-            mt, n = order[unit // 2][0], 2 * order[unit // 2][1] + unit % 2
-            force[unit] = psum.tile([P, NB], F32, name="acc", tag="acc")
-            for g in range(G):
+        def multiply_force(unit, passes=range(G)):
+            mt, nh, j = place(unit)
+            if unit not in force:
+                force[unit] = bank([P, NB])
+            for g in passes:
+                gh, gl = divmod(g, 2)
                 nc.tensor.matmul_mx(
                     out=force[unit][:],
                     lhsT=x_codes[mt][:, g * P : (g + 1) * P].bitcast(E4M3),
                     lhsT_scale=x_scales[mt][:, g * P : (g + 1) * P],
-                    rhs=c_tiles[n][:, g, :].bitcast(E2M1),
-                    rhs_scale=c_planes[n // 2][:, g, (n % 2) * NB : (n % 2 + 1) * NB],
+                    rhs=c_codes[nh, gh][:, gl, 2 * j * NB : 2 * (j + 1) * NB].bitcast(E2M1),
+                    rhs_scale=c_planes[nh, gh][:, gl, j * NB : (j + 1) * NB],
                     start=(g == 0),
                     stop=(g == G - 1),
                 )
 
         def infect(unit):
-            mt, n = order[unit // 2][0], 2 * order[unit // 2][1] + unit % 2
-            infected[unit] = work.tile([P, PACK, P], F32, name="infected", tag="infected", bufs=4)
+            mt, nh, j = place(unit)
+            infected[unit] = work.tile([P, PACK, P], F32, name="infected", tag="infected", bufs=6)
             nc.vector.tensor_tensor(
-                out=infected[unit][:].rearrange("p t (a i) -> p a t i", i=2),
-                in0=force[unit][:].rearrange("p (a i t) -> p a t i", i=2, t=PACK),
-                in1=sus[mt][:, n * NB : (n + 1) * NB].rearrange("p (a i t) -> p a t i", i=2, t=PACK),
+                out=infected[unit][:].rearrange("p t (a i) -> p a t i", i=4),
+                in0=force[unit][:].rearrange("p (a i t) -> p a t i", i=4, t=PACK),
+                in1=sus[mt // 2, nh][:, mt % 2, j * NB : (j + 1) * NB].rearrange("p (a i t) -> p a t i", i=4, t=PACK),
                 op=ALU.mult,
             )
 
         def turn(unit):
-            turned[unit] = psum.tile([P, PACK, P], F32, name="turn", tag="turn")
+            turned[unit] = bank([P, PACK, P])
             for t in range(PACK):
                 nc.tensor.transpose(turned[unit][:, t, :], infected[unit][:, t, :], ident[:])
 
         def subtract(unit):
-            pair, g = divmod(unit, 2)
-            if g == 0:
-                d_pair[pair] = work.tile([P, 2, P, PACK], BF16, name="d_pair", tag="d_pair", align_bytes=64)
+            mt, nh, j = place(unit)
+            if j == 0:
+                d_pair[mt, nh] = work.tile([P, 2, P, PACK], BF16, name="d_pair", tag="d_pair", align_bytes=64)
             nc.vector.tensor_tensor(
-                out=d_pair[pair][:, g, :, :].rearrange("p (a i) t -> p a t i", i=2),
+                out=d_pair[mt, nh][:, j, :, :].rearrange("p (a i) t -> p a t i", i=2),
                 in0=turned[unit][:].rearrange("p t (a i) -> p a t i", i=2),
-                in1=recovered[pair][:, g, :, :].rearrange("p t (a i) -> p a t i", i=2),
+                in1=recovered[mt][nh][:, j, :, :].rearrange("p t (a i) -> p a t i", i=2),
                 op=ALU.subtract,
             )
 
         def quantize_d(pair):
-            mt, half = order[pair]
-            cols = slice(half * 2 * P, (half + 1) * 2 * P)
+            nh, mt = divmod(pair, MT)
+            cols = slice(nh * 2 * P, (nh + 1) * 2 * P)
             nc.vector.quantize_mx(
                 out=d_codes[mt][:, cols].bitcast(E5M2),
                 scales=d_scales[mt][:, cols],
-                in_=d_pair[pair][:].rearrange("p a m t -> p (a m t)"),
+                in_=d_pair[mt, nh][:].rearrange("p a m t -> p (a m t)"),
             )
 
         def group_w(h, g):
             w_grouped[h, g] = work.tile([P, NB, PACK], BF16, name="w_grouped", tag="w_grouped", align_bytes=64, bufs=4)
             nc.scalar.copy(
                 out=w_grouped[h, g][:].rearrange("p (c i) t -> p c t i", i=4),
-                in_=w_raw[h][g][:].rearrange("p t (c i) -> p c t i", i=4),
+                in_=w_raw[g][:, :, h * NB : (h + 1) * NB].rearrange("p t (c i) -> p c t i", i=4),
             )
 
         def quantize_w(h, g):
             nc.vector.quantize_mx(
-                out=w_codes[h][g][:].bitcast(E4M3),
-                scales=w_scales[h][g][:],
+                out=w_codes[h, g][:].bitcast(E4M3),
+                scales=w_scales[h, g][:],
                 in_=w_grouped[h, g][:].rearrange("p c t -> p (c t)"),
             )
 
-        def multiply_out(h, mt):
-            tag = "acc" if h == 0 else "turn"
-            scores[h, mt] = psum.tile([P, NB], F32, name=tag, tag=tag)
-            for g in range(G):
+        def multiply_out(h, mt, passes=range(G)):
+            if (h, mt) not in scores:
+                scores[h, mt] = bank([P, NB])
+            for g in passes:
                 nc.tensor.matmul_mx(
                     out=scores[h, mt][:],
                     lhsT=d_codes[mt][:, g * P : (g + 1) * P].bitcast(E5M2),
                     lhsT_scale=d_scales[mt][:, g * P : (g + 1) * P],
-                    rhs=w_codes[h][g][:].bitcast(E4M3),
-                    rhs_scale=w_scales[h][g][:],
+                    rhs=w_codes[h, g][:].bitcast(E4M3),
+                    rhs_scale=w_scales[h, g][:],
                     start=(g == 0),
                     stop=(g == G - 1),
                 )
@@ -231,81 +230,117 @@ def tile_malware_outbreak_readout_s9_kernel(tc, x, c_words, c_scales, susceptibl
             width = NB // pieces
             for c in range(0, NB, width):
                 cols = slice(h * NB + c, h * NB + c + width)
-                result = work.tile([P, width], F32, name="result", tag="result", bufs=9)
+                result = work.tile([P, width], F32, name="result", tag="result", bufs=8)
                 nc.vector.tensor_tensor(out=result[:], in0=scores[h, mt][:, c : c + width], in1=bias[:, cols], op=ALU.add)
                 nc.sync.dma_start(out=out[mt * P : (mt + 1) * P, cols], in_=result[:])
 
-        w_parts = [(h, g) for h in range(RH) for g in range(G)]
-        pairs = 2 * MT
-        turn_x(0, 0)
-        turn_x(0, 1)
-        empty_x(0, 0, True)
-        empty_x(0, 1)
-        quantize_x(0, 0)
-        quantize_x(0, 1)
-        recover(0)
+        on_vector = nc.vector.tensor_copy
+        on_scalar = nc.scalar.copy
 
-        turn_x(1, 0)
-        turn_x(1, 1)
-        empty_x(1, 0, True)
-        empty_x(1, 1)
-        quantize_x(1, 0)
-        quantize_x(1, 1)
-        recover(1)
-        recover(2)
-        multiply_force(0)
-        scalar_work = ["w0 r3", "w1", "e r4", "w2 r5", "w3 e", "r6 w4", "r7 w5", "w6"]
-        w_ready = [[], [], [0], [1], [2], [], [3], [], [4], [5, 6]]
-        for j in range(pairs):
-            next_x = {2: 2, 4: 3}.get(j)
-            if j > 0:
-                multiply_force(2 * j)
-            multiply_force(2 * j + 1)
-            if j >= 1:
-                turn(2 * j - 2)
-                turn(2 * j - 1)
-            if next_x:
-                turn_x(next_x, 0)
-                turn_x(next_x, 1)
-            infect(2 * j)
-            if j in (3, 5):
-                quantize_x(j // 2 + 1, 0)
-                quantize_x(j // 2 + 1, 1)
-            if j >= 2:
-                quantize_d(j - 2)
-            for k in w_ready[j]:
-                quantize_w(*w_parts[k])
-            infect(2 * j + 1)
-            if j >= 1:
-                subtract(2 * j - 2)
-                subtract(2 * j - 1)
-            for item in scalar_work[j].split():
-                if item[0] == "w":
-                    group_w(*w_parts[int(item[1])])
-                elif item[0] == "r":
-                    recover(int(item[1]))
-                else:
-                    empty_x(next_x, 0)
-                    empty_x(next_x, 1)
+        turn_x(0)
+        for half in range(2):
+            empty_x(0, half, on_vector)
+            quantize_x(0, half)
+        recover(0, 0)
+        recover(0, 1)
+        for unit in (0, 1):
+            multiply_force(unit, range(0, 2))
+        turn_x(1)
+        empty_x(1, 0, on_vector)
+        empty_x(1, 1, on_scalar)
+        for half in range(2):
+            quantize_x(1, half)
+        recover(1, 0)
+        recover(1, 1)
+        for unit in (0, 1):
+            multiply_force(unit, range(2, G))
+        turn_x(2)
+        infect(0)
+        infect(1)
+        for half in range(2):
+            empty_x(2, half, on_vector)
+        recover(2, 0)
+        recover(2, 1)
+        multiply_force(2)
+        multiply_force(3)
+        quantize_x(2, 0)
+        quantize_x(2, 1)
+        infect(2)
+        infect(3)
+        turn_x(3)
+        turn(0)
+        turn(1)
+        empty_x(3, 0, on_vector)
+        empty_x(3, 1, on_scalar)
+        group_w(0, 0)
+        group_w(1, 0)
+        recover(3, 0)
+        for unit in range(4, 6):
+            multiply_force(unit)
+        subtract(0)
+        quantize_x(3, 0)
+        quantize_x(3, 1)
+        for unit in range(6, 8):
+            multiply_force(unit)
+        subtract(1)
+        infect(4)
+        quantize_d(0)
+        infect(5)
+        quantize_w(0, 0)
+        infect(6)
+
+        def round_of_four(u, first_w, second_w):
+            infect(u - 1)
+            for unit in range(u - 6, u - 2):
+                turn(unit)
+            for unit in range(u, u + 4):
+                multiply_force(unit)
+            subtract(u - 6)
+            subtract(u - 5)
+            quantize_w(*first_w)
+            subtract(u - 4)
+            quantize_d((u - 6) // 2)
+            subtract(u - 3)
+            infect(u)
+            quantize_d((u - 4) // 2)
+            infect(u + 1)
+            quantize_w(*second_w)
+            infect(u + 2)
+
+        group_w(0, 1)
+        round_of_four(8, (1, 0), (0, 1))
+        group_w(0, 2)
+        group_w(0, 3)
+        recover(3, 1)
+        round_of_four(12, (0, 2), (0, 3))
+        for g in range(1, G):
+            group_w(1, g)
+        infect(15)
+        for unit in range(10, 16):
+            turn(unit)
         multiply_out(0, 0)
+        subtract(10)
+        subtract(11)
+        subtract(12)
+        quantize_d(5)
         multiply_out(0, 1)
-        turn(2 * pairs - 2)
-        turn(2 * pairs - 1)
-        quantize_d(pairs - 2)
-        for k in w_ready[8]:
-            quantize_w(*w_parts[k])
-        group_w(*w_parts[7])
-        subtract(2 * pairs - 2)
-        subtract(2 * pairs - 1)
-        store(0, 0)
-        quantize_d(pairs - 1)
+        subtract(13)
+        subtract(14)
+        quantize_d(6)
         multiply_out(0, 2)
+        subtract(15)
+        quantize_w(1, 1)
+        quantize_d(7)
         multiply_out(0, 3)
-        for k in w_ready[9]:
-            quantize_w(*w_parts[k])
+        quantize_w(1, 2)
+        store(0, 0)
         store(0, 1)
-        quantize_w(*w_parts[7])
-        for mt in range(MT):
+        for mt in range(2):
+            multiply_out(1, mt, range(G - 1))
+        quantize_w(1, 3)
+        for mt in range(2):
+            multiply_out(1, mt, range(G - 1, G))
+        for mt in range(2, MT):
             multiply_out(1, mt)
         for mt in range(2, MT):
             store(0, mt)

@@ -25,6 +25,8 @@ MT = M // P
 NB = 512
 RH = R // NB
 HALF = H // 2
+LINE = 4
+BANKS = 8
 
 
 def tile_malware_outbreak_readout_s9_kernel(tc, x, c_words, c_scales, susceptible, recovery, w, b, out):
@@ -32,24 +34,25 @@ def tile_malware_outbreak_readout_s9_kernel(tc, x, c_words, c_scales, susceptibl
     with ExitStack() as ctx:
         keep = ctx.enter_context(tc.tile_pool(name="keep", bufs=1))
         work = ctx.enter_context(tc.tile_pool(name="work", bufs=3))
-        psum = ctx.enter_context(tc.psum_pool(name="psum", bufs=8))
+        psum = ctx.enter_context(tc.psum_pool(name="psum", bufs=BANKS))
         ctx.enter_context(tc.manual_schedule())
 
         def kept(name, shape, dtype):
             return keep.tile(shape, dtype, name=name, align_bytes=64)
 
+        halves = range(2)
         ident = kept("ident", [P, P], F32)
         rec_raw = kept("rec_raw", [P, G * PACK], BF16)
         rec = kept("rec", [P, G * PACK], F32)
         bias = kept("bias", [P, R], BF16)
-        c_codes = {(nh, gh): kept("c_%d_%d" % (nh, gh), [P, 2, 2 * HALF], U8) for nh in range(2) for gh in range(2)}
-        c_planes = {(nh, gh): kept("cs_%d_%d" % (nh, gh), [P, 2, HALF], U8) for nh in range(2) for gh in range(2)}
-        x_first = [kept("x0_%d" % h, [P, HALF], BF16) for h in range(2)]
+        c_codes = {(nh, gh): kept("c_%d_%d" % (nh, gh), [P, 2, 2 * HALF], U8) for nh in halves for gh in halves}
+        c_planes = {(nh, gh): kept("cs_%d_%d" % (nh, gh), [P, 2, HALF], U8) for nh in halves for gh in halves}
+        x_first = [kept("x0_%d" % half, [P, HALF], BF16) for half in halves]
         x_rest = [kept("x_%d" % mt, [P, H], BF16) for mt in range(1, MT)]
-        sus = {(mp, nh): kept("sus_%d_%d" % (mp, nh), [P, 2, HALF], BF16) for nh in range(2) for mp in range(2)}
+        sus = {(mp, nh): kept("sus_%d_%d" % (mp, nh), [P, 2, HALF], BF16) for nh in halves for mp in halves}
         w_raw = [kept("w_%d" % g, [P, PACK, R], BF16) for g in range(G)]
-        xt = [[kept("xt_%d_%d" % (mt, h), [P, HALF], BF16) for h in range(2)] for mt in range(MT)]
-        recovered = [[kept("rx_%d_%d" % (mt, h), [P, 2, PACK, P], F32) for h in range(2)] for mt in range(MT)]
+        xt = [[kept("xt_%d_%d" % (mt, half), [P, HALF], BF16) for half in halves] for mt in range(MT)]
+        recovered = [[kept("rx_%d_%d" % (mt, half), [P, 2, P // LINE, PACK, LINE], F32) for half in halves] for mt in range(MT)]
         x_codes = [kept("xc_%d" % mt, [P, G * P], U32) for mt in range(MT)]
         x_scales = [kept("xs_%d" % mt, [P, G * P], U8) for mt in range(MT)]
         d_codes = [kept("dc_%d" % mt, [P, G * P], U32) for mt in range(MT)]
@@ -83,8 +86,8 @@ def tile_malware_outbreak_readout_s9_kernel(tc, x, c_words, c_scales, susceptibl
         def load_w(g):
             nc.sync.dma_start(out=w_raw[g][:], in_=w[g * KP : (g + 1) * KP, :].rearrange("(p t) c -> p t c", t=PACK))
 
-        for h in range(2):
-            nc.sync.dma_start(out=x_first[h][:], in_=x[0:P, h * HALF : (h + 1) * HALF])
+        for half in halves:
+            nc.sync.dma_start(out=x_first[half][:], in_=x[0:P, half * HALF : (half + 1) * HALF])
         nc.sync.dma_start(out=rec_raw[:].rearrange("p (g t) -> p g t", t=PACK), in_=recovery.rearrange("(g p t) -> p g t", p=P, t=PACK))
         load_c(0, 0)
         load_x(1)
@@ -105,6 +108,7 @@ def tile_malware_outbreak_readout_s9_kernel(tc, x, c_words, c_scales, susceptibl
 
         nc.scalar.activation(out=rec[:], in_=rec_raw[:], func=COPY)
 
+        x_sorted = {}
         turned_x = {}
         force = {}
         infected = {}
@@ -121,14 +125,21 @@ def tile_malware_outbreak_readout_s9_kernel(tc, x, c_words, c_scales, susceptibl
             nh, mt = divmod(pair, MT)
             return mt, nh, j
 
+        def sort_x(mt):
+            x_sorted[mt] = kept("x_sorted", [P, G, 2, P], F32)
+            nc.vector.tensor_copy(out=x_sorted[mt][:], in_=x_rest[mt - 1][:].bitcast(F32).rearrange("m (g p u) -> m g u p", g=G, u=2))
+
         def turn_x(mt):
-            for half in range(2):
-                src = x_first[half][:] if mt == 0 else x_rest[mt - 1][:, half * HALF : (half + 1) * HALF]
-                words = src.bitcast(F32)
+            for half in halves:
+                if mt in x_sorted:
+                    words = x_sorted[mt][:, 2 * half : 2 * half + 2, :, :]
+                else:
+                    rows = x_first[half][:] if mt == 0 else x_rest[mt - 1][:, half * HALF : (half + 1) * HALF]
+                    words = rows.bitcast(F32).rearrange("m (g p u) -> m g u p", g=2, u=2)
                 turned_x[mt, half] = bank([P, 2, 2, P])
                 for g in range(2):
                     for u in range(2):
-                        nc.tensor.transpose(turned_x[mt, half][:, g, u, :], words[:, 256 * g + u : 256 * (g + 1) : 2], ident[:])
+                        nc.tensor.transpose(turned_x[mt, half][:, g, u, :], words[:, g, u, :], ident[:])
 
         def empty_x(mt, half, copy):
             copy(
@@ -141,11 +152,11 @@ def tile_malware_outbreak_readout_s9_kernel(tc, x, c_words, c_scales, susceptibl
             nc.vector.quantize_mx(out=x_codes[mt][:, cols].bitcast(E4M3), scales=x_scales[mt][:, cols], in_=xt[mt][half][:])
 
         def recover(mt, half):
-            src = xt[mt][half][:].rearrange("p (g m t) -> p g t m", g=2, t=PACK)
+            values = xt[mt][half][:].rearrange("p (g a i t) -> p g t a i", g=2, i=LINE, t=PACK)
             for g in range(2):
                 for t in range(PACK):
-                    j = (2 * half + g) * PACK + t
-                    nc.scalar.activation(out=recovered[mt][half][:, g, t, :], in_=src[:, g, t, :], func=COPY, scale=rec[:, j : j + 1])
+                    col = (2 * half + g) * PACK + t
+                    nc.scalar.activation(out=recovered[mt][half][:, g, :, t, :], in_=values[:, g, t, :, :], func=COPY, scale=rec[:, col : col + 1])
 
         def multiply_force(unit, passes=range(G)):
             mt, nh, j = place(unit)
@@ -167,9 +178,9 @@ def tile_malware_outbreak_readout_s9_kernel(tc, x, c_words, c_scales, susceptibl
             mt, nh, j = place(unit)
             infected[unit] = work.tile([P, PACK, P], F32, name="infected", tag="infected", bufs=6)
             nc.vector.tensor_tensor(
-                out=infected[unit][:].rearrange("p t (a i) -> p a t i", i=4),
-                in0=force[unit][:].rearrange("p (a i t) -> p a t i", i=4, t=PACK),
-                in1=sus[mt // 2, nh][:, mt % 2, j * NB : (j + 1) * NB].rearrange("p (a i t) -> p a t i", i=4, t=PACK),
+                out=infected[unit][:].rearrange("m t (a i) -> m a t i", i=LINE),
+                in0=force[unit][:].rearrange("m (a i t) -> m a t i", i=LINE, t=PACK),
+                in1=sus[mt // 2, nh][:, mt % 2, j * NB : (j + 1) * NB].rearrange("m (a i t) -> m a t i", i=LINE, t=PACK),
                 op=ALU.mult,
             )
 
@@ -183,9 +194,9 @@ def tile_malware_outbreak_readout_s9_kernel(tc, x, c_words, c_scales, susceptibl
             if j == 0:
                 d_pair[mt, nh] = work.tile([P, 2, P, PACK], BF16, name="d_pair", tag="d_pair", align_bytes=64)
             nc.vector.tensor_tensor(
-                out=d_pair[mt, nh][:, j, :, :].rearrange("p (a i) t -> p a t i", i=2),
-                in0=turned[unit][:].rearrange("p t (a i) -> p a t i", i=2),
-                in1=recovered[mt][nh][:, j, :, :].rearrange("p t (a i) -> p a t i", i=2),
+                out=d_pair[mt, nh][:, j, :, :].rearrange("p (a i) t -> p a t i", i=LINE),
+                in0=turned[unit][:].rearrange("p t (a i) -> p a t i", i=LINE),
+                in1=recovered[mt][nh][:, j, :, :, :],
                 op=ALU.subtract,
             )
 
@@ -201,8 +212,8 @@ def tile_malware_outbreak_readout_s9_kernel(tc, x, c_words, c_scales, susceptibl
         def group_w(h, g):
             w_grouped[h, g] = work.tile([P, NB, PACK], BF16, name="w_grouped", tag="w_grouped", align_bytes=64, bufs=4)
             nc.scalar.copy(
-                out=w_grouped[h, g][:].rearrange("p (c i) t -> p c t i", i=4),
-                in_=w_raw[g][:, :, h * NB : (h + 1) * NB].rearrange("p t (c i) -> p c t i", i=4),
+                out=w_grouped[h, g][:].rearrange("p (c i) t -> p c t i", i=LINE),
+                in_=w_raw[g][:, :, h * NB : (h + 1) * NB].rearrange("p t (c i) -> p c t i", i=LINE),
             )
 
         def quantize_w(h, g):
@@ -238,17 +249,18 @@ def tile_malware_outbreak_readout_s9_kernel(tc, x, c_words, c_scales, susceptibl
         on_scalar = nc.scalar.copy
 
         turn_x(0)
-        for half in range(2):
+        for half in halves:
             empty_x(0, half, on_vector)
             quantize_x(0, half)
         recover(0, 0)
         recover(0, 1)
         for unit in (0, 1):
             multiply_force(unit, range(0, 2))
+        sort_x(1)
         turn_x(1)
         empty_x(1, 0, on_vector)
         empty_x(1, 1, on_scalar)
-        for half in range(2):
+        for half in halves:
             quantize_x(1, half)
         recover(1, 0)
         recover(1, 1)
@@ -257,7 +269,7 @@ def tile_malware_outbreak_readout_s9_kernel(tc, x, c_words, c_scales, susceptibl
         turn_x(2)
         infect(0)
         infect(1)
-        for half in range(2):
+        for half in halves:
             empty_x(2, half, on_vector)
         recover(2, 0)
         recover(2, 1)
@@ -275,13 +287,13 @@ def tile_malware_outbreak_readout_s9_kernel(tc, x, c_words, c_scales, susceptibl
         group_w(0, 0)
         group_w(1, 0)
         recover(3, 0)
-        for unit in range(4, 6):
-            multiply_force(unit)
+        multiply_force(4)
+        multiply_force(5)
         subtract(0)
         quantize_x(3, 0)
         quantize_x(3, 1)
-        for unit in range(6, 8):
-            multiply_force(unit)
+        multiply_force(6)
+        multiply_force(7)
         subtract(1)
         infect(4)
         quantize_d(0)
@@ -315,6 +327,7 @@ def tile_malware_outbreak_readout_s9_kernel(tc, x, c_words, c_scales, susceptibl
         round_of_four(12, (0, 2), (0, 3))
         for g in range(1, G):
             group_w(1, g)
+
         infect(15)
         for unit in range(10, 16):
             turn(unit)
@@ -337,7 +350,7 @@ def tile_malware_outbreak_readout_s9_kernel(tc, x, c_words, c_scales, susceptibl
         store(0, 1)
         for mt in range(2):
             multiply_out(1, mt, range(G - 1))
-        quantize_w(1, 3)
+        quantize_w(1, G - 1)
         for mt in range(2):
             multiply_out(1, mt, range(G - 1, G))
         for mt in range(2, MT):

from contextlib import ExitStack

import concourse.mybir as mybir
from concourse.masks import make_identity

M, H, R = 512, 2048, 1024
FLOPS = 2 * M * H * H + 2 * M * H * R

F32 = mybir.dt.float32
BF16 = mybir.dt.bfloat16
I32 = mybir.dt.int32
U32 = mybir.dt.uint32
U8 = mybir.dt.uint8
E4M3 = mybir.dt.float8_e4m3fn_x4
E5M2 = mybir.dt.float8_e5m2_x4
E2M1 = mybir.dt.float4_e2m1fn_x4
ALU = mybir.AluOpType
COPY = mybir.ActivationFunctionType.Copy

P = 128
PACK = 4
KP = P * PACK
G = H // KP
MT = M // P
NB = 512
RH = R // NB
HALF = H // 2
LINE = 4
BANKS = 8


def tile_malware_outbreak_readout_s9_kernel(tc, x, c_words, c_scales, susceptible, recovery, w, b, out):
    nc = tc.nc
    with ExitStack() as ctx:
        keep = ctx.enter_context(tc.tile_pool(name="keep", bufs=1))
        work = ctx.enter_context(tc.tile_pool(name="work", bufs=3))
        psum = ctx.enter_context(tc.psum_pool(name="psum", bufs=BANKS))
        ctx.enter_context(tc.manual_schedule())

        def kept(name, shape, dtype):
            return keep.tile(shape, dtype, name=name, align_bytes=64)

        halves = range(2)
        ident = kept("ident", [P, P], F32)
        rec_raw = kept("rec_raw", [P, G * PACK], BF16)
        rec = kept("rec", [P, G * PACK], F32)
        bias = kept("bias", [P, R], BF16)
        c_codes = {(nh, gh): kept("c_%d_%d" % (nh, gh), [P, 2, 2 * HALF], U8) for nh in halves for gh in halves}
        c_planes = {(nh, gh): kept("cs_%d_%d" % (nh, gh), [P, 2, HALF], U8) for nh in halves for gh in halves}
        x_first = [kept("x0_%d" % half, [P, HALF], BF16) for half in halves]
        x_rest = [kept("x_%d" % mt, [P, H], BF16) for mt in range(1, MT)]
        sus = {(mp, nh): kept("sus_%d_%d" % (mp, nh), [P, 2, HALF], BF16) for nh in halves for mp in halves}
        w_raw = [kept("w_%d" % g, [P, PACK, R], BF16) for g in range(G)]
        xt = [[kept("xt_%d_%d" % (mt, half), [P, HALF], BF16) for half in halves] for mt in range(MT)]
        recovered = [[kept("rx_%d_%d" % (mt, half), [P, 2, P // LINE, PACK, LINE], F32) for half in halves] for mt in range(MT)]
        x_codes = [kept("xc_%d" % mt, [P, G * P], U32) for mt in range(MT)]
        x_scales = [kept("xs_%d" % mt, [P, G * P], U8) for mt in range(MT)]
        d_codes = [kept("dc_%d" % mt, [P, G * P], U32) for mt in range(MT)]
        d_scales = [kept("ds_%d" % mt, [P, G * P], U8) for mt in range(MT)]
        w_codes = {(h, g): kept("wc_%d_%d" % (h, g), [P, NB], U32) for h in range(RH) for g in range(G)}
        w_scales = {(h, g): kept("ws_%d_%d" % (h, g), [P, NB], U8) for h in range(RH) for g in range(G)}

        for plane in c_planes.values():
            nc.vector.memset(plane[:].bitcast(I32), 0)
        make_identity(nc, ident[:])

        scale_rows = c_scales.bitcast(I32).rearrange("g (q r) n -> r q g n", r=4)
        c_view = c_words.bitcast(I32).rearrange("g p n -> p g n")

        def load_c(nh, gh):
            gs = slice(2 * gh, 2 * gh + 2)
            for r in range(4):
                nc.sync.dma_start(
                    out=c_planes[nh, gh][r:P:32, :, :].bitcast(I32),
                    in_=scale_rows[r, :, gs, nh * HALF // 4 : (nh + 1) * HALF // 4],
                )
            nc.sync.dma_start(out=c_codes[nh, gh][:].bitcast(I32), in_=c_view[:, gs, nh * HALF // 2 : (nh + 1) * HALF // 2])

        def load_x(mt):
            nc.sync.dma_start(out=x_rest[mt - 1][:], in_=x[mt * P : (mt + 1) * P, :])

        def load_sus(mp, nh):
            rows = susceptible[2 * mp * P : 2 * (mp + 1) * P, nh * HALF : (nh + 1) * HALF]
            nc.sync.dma_start(out=sus[mp, nh][:], in_=rows.rearrange("(a p) c -> p a c", p=P))

        def load_w(g):
            nc.sync.dma_start(out=w_raw[g][:], in_=w[g * KP : (g + 1) * KP, :].rearrange("(p t) c -> p t c", t=PACK))

        for half in halves:
            nc.sync.dma_start(out=x_first[half][:], in_=x[0:P, half * HALF : (half + 1) * HALF])
        nc.sync.dma_start(out=rec_raw[:].rearrange("p (g t) -> p g t", t=PACK), in_=recovery.rearrange("(g p t) -> p g t", p=P, t=PACK))
        load_c(0, 0)
        load_x(1)
        load_c(0, 1)
        load_x(2)
        load_sus(0, 0)
        load_x(3)
        load_w(0)
        load_sus(1, 0)
        load_c(1, 0)
        load_c(1, 1)
        load_w(1)
        load_sus(0, 1)
        load_w(2)
        load_w(3)
        load_sus(1, 1)
        nc.sync.dma_start(out=bias[:], in_=b.partition_broadcast(P))

        nc.scalar.activation(out=rec[:], in_=rec_raw[:], func=COPY)

        x_sorted = {}
        turned_x = {}
        force = {}
        infected = {}
        turned = {}
        d_pair = {}
        w_grouped = {}
        scores = {}

        def bank(shape):
            return psum.tile(shape, F32, name="bank", tag="bank")

        def place(unit):
            pair, j = divmod(unit, 2)
            nh, mt = divmod(pair, MT)
            return mt, nh, j

        def sort_x(mt):
            x_sorted[mt] = kept("x_sorted", [P, G, 2, P], F32)
            nc.vector.tensor_copy(out=x_sorted[mt][:], in_=x_rest[mt - 1][:].bitcast(F32).rearrange("m (g p u) -> m g u p", g=G, u=2))

        def turn_x(mt):
            for half in halves:
                if mt in x_sorted:
                    words = x_sorted[mt][:, 2 * half : 2 * half + 2, :, :]
                else:
                    rows = x_first[half][:] if mt == 0 else x_rest[mt - 1][:, half * HALF : (half + 1) * HALF]
                    words = rows.bitcast(F32).rearrange("m (g p u) -> m g u p", g=2, u=2)
                turned_x[mt, half] = bank([P, 2, 2, P])
                for g in range(2):
                    for u in range(2):
                        nc.tensor.transpose(turned_x[mt, half][:, g, u, :], words[:, g, u, :], ident[:])

        def empty_x(mt, half, copy):
            copy(
                out=xt[mt][half][:].bitcast(F32).rearrange("p (g m u) -> p g m u", g=2, u=2),
                in_=turned_x[mt, half][:].rearrange("p g u m -> p g m u"),
            )

        def quantize_x(mt, half):
            cols = slice(half * 2 * P, (half + 1) * 2 * P)
            nc.vector.quantize_mx(out=x_codes[mt][:, cols].bitcast(E4M3), scales=x_scales[mt][:, cols], in_=xt[mt][half][:])

        def recover(mt, half):
            values = xt[mt][half][:].rearrange("p (g a i t) -> p g t a i", g=2, i=LINE, t=PACK)
            for g in range(2):
                for t in range(PACK):
                    col = (2 * half + g) * PACK + t
                    nc.scalar.activation(out=recovered[mt][half][:, g, :, t, :], in_=values[:, g, t, :, :], func=COPY, scale=rec[:, col : col + 1])

        def multiply_force(unit, passes=range(G)):
            mt, nh, j = place(unit)
            if unit not in force:
                force[unit] = bank([P, NB])
            for g in passes:
                gh, gl = divmod(g, 2)
                nc.tensor.matmul_mx(
                    out=force[unit][:],
                    lhsT=x_codes[mt][:, g * P : (g + 1) * P].bitcast(E4M3),
                    lhsT_scale=x_scales[mt][:, g * P : (g + 1) * P],
                    rhs=c_codes[nh, gh][:, gl, 2 * j * NB : 2 * (j + 1) * NB].bitcast(E2M1),
                    rhs_scale=c_planes[nh, gh][:, gl, j * NB : (j + 1) * NB],
                    start=(g == 0),
                    stop=(g == G - 1),
                )

        def infect(unit):
            mt, nh, j = place(unit)
            infected[unit] = work.tile([P, PACK, P], F32, name="infected", tag="infected", bufs=6)
            nc.vector.tensor_tensor(
                out=infected[unit][:].rearrange("m t (a i) -> m a t i", i=LINE),
                in0=force[unit][:].rearrange("m (a i t) -> m a t i", i=LINE, t=PACK),
                in1=sus[mt // 2, nh][:, mt % 2, j * NB : (j + 1) * NB].rearrange("m (a i t) -> m a t i", i=LINE, t=PACK),
                op=ALU.mult,
            )

        def turn(unit):
            turned[unit] = bank([P, PACK, P])
            for t in range(PACK):
                nc.tensor.transpose(turned[unit][:, t, :], infected[unit][:, t, :], ident[:])

        def subtract(unit):
            mt, nh, j = place(unit)
            if j == 0:
                d_pair[mt, nh] = work.tile([P, 2, P, PACK], BF16, name="d_pair", tag="d_pair", align_bytes=64)
            nc.vector.tensor_tensor(
                out=d_pair[mt, nh][:, j, :, :].rearrange("p (a i) t -> p a t i", i=LINE),
                in0=turned[unit][:].rearrange("p t (a i) -> p a t i", i=LINE),
                in1=recovered[mt][nh][:, j, :, :, :],
                op=ALU.subtract,
            )

        def quantize_d(pair):
            nh, mt = divmod(pair, MT)
            cols = slice(nh * 2 * P, (nh + 1) * 2 * P)
            nc.vector.quantize_mx(
                out=d_codes[mt][:, cols].bitcast(E5M2),
                scales=d_scales[mt][:, cols],
                in_=d_pair[mt, nh][:].rearrange("p a m t -> p (a m t)"),
            )

        def group_w(h, g):
            w_grouped[h, g] = work.tile([P, NB, PACK], BF16, name="w_grouped", tag="w_grouped", align_bytes=64, bufs=4)
            nc.scalar.copy(
                out=w_grouped[h, g][:].rearrange("p (c i) t -> p c t i", i=LINE),
                in_=w_raw[g][:, :, h * NB : (h + 1) * NB].rearrange("p t (c i) -> p c t i", i=LINE),
            )

        def quantize_w(h, g):
            nc.vector.quantize_mx(
                out=w_codes[h, g][:].bitcast(E4M3),
                scales=w_scales[h, g][:],
                in_=w_grouped[h, g][:].rearrange("p c t -> p (c t)"),
            )

        def multiply_out(h, mt, passes=range(G)):
            if (h, mt) not in scores:
                scores[h, mt] = bank([P, NB])
            for g in passes:
                nc.tensor.matmul_mx(
                    out=scores[h, mt][:],
                    lhsT=d_codes[mt][:, g * P : (g + 1) * P].bitcast(E5M2),
                    lhsT_scale=d_scales[mt][:, g * P : (g + 1) * P],
                    rhs=w_codes[h, g][:].bitcast(E4M3),
                    rhs_scale=w_scales[h, g][:],
                    start=(g == 0),
                    stop=(g == G - 1),
                )

        def store(h, mt, pieces=1):
            width = NB // pieces
            for c in range(0, NB, width):
                cols = slice(h * NB + c, h * NB + c + width)
                result = work.tile([P, width], F32, name="result", tag="result", bufs=8)
                nc.vector.tensor_tensor(out=result[:], in0=scores[h, mt][:, c : c + width], in1=bias[:, cols], op=ALU.add)
                nc.sync.dma_start(out=out[mt * P : (mt + 1) * P, cols], in_=result[:])

        on_vector = nc.vector.tensor_copy
        on_scalar = nc.scalar.copy

        turn_x(0)
        for half in halves:
            empty_x(0, half, on_vector)
            quantize_x(0, half)
        recover(0, 0)
        recover(0, 1)
        for unit in (0, 1):
            multiply_force(unit, range(0, 2))
        sort_x(1)
        turn_x(1)
        empty_x(1, 0, on_vector)
        empty_x(1, 1, on_scalar)
        for half in halves:
            quantize_x(1, half)
        recover(1, 0)
        recover(1, 1)
        for unit in (0, 1):
            multiply_force(unit, range(2, G))
        turn_x(2)
        infect(0)
        infect(1)
        for half in halves:
            empty_x(2, half, on_vector)
        recover(2, 0)
        recover(2, 1)
        multiply_force(2)
        multiply_force(3)
        quantize_x(2, 0)
        quantize_x(2, 1)
        infect(2)
        infect(3)
        turn_x(3)
        turn(0)
        turn(1)
        empty_x(3, 0, on_vector)
        empty_x(3, 1, on_scalar)
        group_w(0, 0)
        group_w(1, 0)
        recover(3, 0)
        multiply_force(4)
        multiply_force(5)
        subtract(0)
        quantize_x(3, 0)
        quantize_x(3, 1)
        multiply_force(6)
        multiply_force(7)
        subtract(1)
        infect(4)
        quantize_d(0)
        infect(5)
        quantize_w(0, 0)
        infect(6)

        def round_of_four(u, first_w, second_w):
            infect(u - 1)
            for unit in range(u - 6, u - 2):
                turn(unit)
            for unit in range(u, u + 4):
                multiply_force(unit)
            subtract(u - 6)
            subtract(u - 5)
            quantize_w(*first_w)
            subtract(u - 4)
            quantize_d((u - 6) // 2)
            subtract(u - 3)
            infect(u)
            quantize_d((u - 4) // 2)
            infect(u + 1)
            quantize_w(*second_w)
            infect(u + 2)

        group_w(0, 1)
        round_of_four(8, (1, 0), (0, 1))
        group_w(0, 2)
        group_w(0, 3)
        recover(3, 1)
        round_of_four(12, (0, 2), (0, 3))
        for g in range(1, G):
            group_w(1, g)

        infect(15)
        for unit in range(10, 16):
            turn(unit)
        multiply_out(0, 0)
        subtract(10)
        subtract(11)
        subtract(12)
        quantize_d(5)
        multiply_out(0, 1)
        subtract(13)
        subtract(14)
        quantize_d(6)
        multiply_out(0, 2)
        subtract(15)
        quantize_w(1, 1)
        quantize_d(7)
        multiply_out(0, 3)
        quantize_w(1, 2)
        store(0, 0)
        store(0, 1)
        for mt in range(2):
            multiply_out(1, mt, range(G - 1))
        quantize_w(1, G - 1)
        for mt in range(2):
            multiply_out(1, mt, range(G - 1, G))
        for mt in range(2, MT):
            multiply_out(1, mt)
        for mt in range(2, MT):
            store(0, mt)
        for mt in range(MT):
            store(1, mt, 2 if mt == MT - 1 else 1)
